import numpy as np
import ml_dtypes


def mxq(x, axis, fmt="e4m3"):
    dtype, down = {"e4m3": (ml_dtypes.float8_e4m3fn, 7), "e5m2": (ml_dtypes.float8_e5m2, 14)}[fmt]
    v = np.moveaxis(np.asarray(x, np.float32).astype(ml_dtypes.bfloat16).astype(np.float64), axis, -1)
    blocks = v.reshape(v.shape[:-1] + (-1, 32))
    amax = np.abs(blocks).max(-1, keepdims=True)
    byte = np.maximum(np.where(amax > 0, np.frexp(amax)[1] - 1 + 127, 0) - down, 1)
    scale = np.exp2(byte - 127.0)
    codes = (blocks / scale).astype(np.float32).astype(dtype).astype(np.float64)
    return np.moveaxis((codes * scale).reshape(v.shape), -1, axis)


WIDE = False


def mx_kscale(k):
    if not WIDE:
        return np.ones(k)
    levels = np.array([10, -10, 5, -5, 0])
    if k % 512:
        return np.exp2(np.random.permutation(np.resize(levels, k // 32))).repeat(32)
    a = np.empty((k // 512, 16))
    for p in range(k // 512):
        a[p, :8] = np.random.permutation(np.resize(levels, 8))
        for g in range(8):
            far = levels[np.abs(levels - a[p, g]) >= 10]
            a[p, g + 8] = far[np.random.randint(len(far))]
    return np.exp2(a.ravel()).repeat(32)


BF16 = ml_dtypes.bfloat16


def bf(x):
    return np.asarray(x, np.float32).astype(BF16)


def f64(x):
    return np.asarray(x).astype(np.float64)

E4M3FN = np.array([(-1.0 if i & 128 else 1.0) * ((1.0 + (i & 7) / 8.0) * 2.0 ** (((i >> 3) & 15) - 7) if i & 120 else (i & 7) * 2.0 ** -9) for i in range(256)])


def e4m3fn_bytes(y):
    return np.clip(np.asarray(y, np.float64), -448.0, 448.0).astype(np.float32).astype(ml_dtypes.float8_e4m3fn).view(np.uint8)


def e4m3fn_values(b):
    return E4M3FN[b]


N, B, E = 1024, 128, 16


def setup_inputs():
    s = mx_kscale(N)
    a, c = np.random.standard_normal((2, E, N))
    P = sum(v[:, None] * v for v in a) / E * s[:, None] * s
    F = np.random.standard_normal((N, N)) / np.sqrt(N) / s
    Q = 0.3 * sum(v[:, None] * v for v in c) / E
    P_scale = (np.abs(P).reshape(N, N // B, B).max(axis=2) / 448.0).astype(np.float32)
    F_scale = (np.abs(F).reshape(N // B, B, N // B, B).max(axis=(1, 3)) / 448.0).astype(np.float32)
    return {"P_bytes": e4m3fn_bytes(P / np.repeat(f64(P_scale), B, axis=1)),
            "P_scale": P_scale,
            "F_bytes": e4m3fn_bytes(F / np.repeat(np.repeat(f64(F_scale), B, axis=0), B, axis=1)),
            "F_scale": F_scale,
            "g": bf(1 + 0.1 * np.random.standard_normal(N)),
            "Q": bf(Q)}


def reference(P_bytes, P_scale, F_bytes, F_scale, g, Q):
    P = e4m3fn_values(P_bytes) * np.repeat(f64(P_scale), B, axis=1)
    F = e4m3fn_values(F_bytes) * np.repeat(np.repeat(f64(F_scale), B, axis=0), B, axis=1)
    gain = f64(g)
    fq = mxq(F, 1, "e4m3")
    h = (mxq(P, 1, "e4m3") @ fq.T) * gain
    y = fq @ mxq(h, 0, "e4m3")
    return y * gain[:, None] + f64(Q)

@@ -1,0 +1,236 @@
+from contextlib import ExitStack
+
+import concourse.mybir as mybir
+from concourse.masks import make_identity
+
+N = 1024
+P = 128
+FLOPS = 2 * 2 * N * N * N
+
+F32 = mybir.dt.float32
+BF16 = mybir.dt.bfloat16
+U32 = mybir.dt.uint32
+U8 = mybir.dt.uint8
+FP8 = mybir.dt.float8_e4m3fn
+FP8X4 = mybir.dt.float8_e4m3fn_x4
+MULT = mybir.AluOpType.mult
+ADD = mybir.AluOpType.add
+COPY = mybir.ActivationFunctionType.Copy
+
+
+def tile_kalman_predicted_covariance_d2_kernel(tc, P_bytes, P_scale, F_bytes, F_scale, g, Q, out):
+    nc = tc.nc
+    with ExitStack() as ctx:
+        keep = ctx.enter_context(tc.tile_pool(name="keep", bufs=1))
+        psum = ctx.enter_context(tc.psum_pool(name="psum", bufs=8))
+        ctx.enter_context(tc.manual_schedule())
+
+
+        order = [("P", 0), ("P", 1), ("P", 2), ("P", 3), ("F", 0), ("F", 1), ("F", 2), ("F", 3)]
+        order += [("P", 4), ("P", 5), ("P", 6), ("P", 7), ("F", 4), ("F", 5), ("F", 6), ("F", 7)]
+        on_scalar = [order[i] for i in range(1, 16, 4)]
+        on_gpsimd = [(1, 0), (3, 0), (5, 0), (7, 0), (0, 1), (2, 1)]
+
+        p_scale = keep.tile([P, 2, 32], F32, name="p_scale")
+        nc.scalar.dma_start(out=p_scale[:], in_=P_scale.rearrange("(g m t) c -> m g (t c)", g=2, t=4))
+        f_scale = keep.tile([P, 64], F32, name="f_scale")
+        nc.scalar.dma_start(out=f_scale[:], in_=F_scale.rearrange("b c -> (b c)").partition_broadcast(P))
+        p_rows = P_bytes.rearrange("(g m t) j -> g m t j", g=2, t=4)
+        f_rows = F_bytes.rearrange("(b p) j -> p b j", p=P)
+        raw = {}
+        scale = {}
+        for i in range(0, 16, 2):
+            kind, b = order[i]
+            pair = keep.tile([P, 2, N], U8, name="bytes_%s%d" % (kind, b))
+            if kind == "P":
+                nc.sync.dma_start(out=pair[:], in_=p_rows[b // 4][:, b % 4 : b % 4 + 2, :])
+            else:
+                nc.sync.dma_start(out=pair[:], in_=f_rows[:, b : b + 2, :])
+            for j in range(2):
+                raw[order[i + j]] = pair[:, j, :]
+        for b in range(8):
+            scale[("P", b)] = p_scale[:, b // 4, 8 * (b % 4) : 8 * (b % 4) + 8]
+            scale[("F", b)] = f_scale[:, 8 * b : 8 * b + 8]
+        g_rows = keep.tile([P, N], BF16, name="g_rows")
+        nc.sync.dma_start(out=g_rows[:], in_=g.partition_broadcast(P))
+        q_rows = Q.rearrange("(b p) n -> p b n", p=P)
+        q_tiles = []
+        for h in range(4):
+            qt = keep.tile([P, 2, N], BF16, name="q%d" % h)
+            nc.sync.dma_start(out=qt[:], in_=q_rows[:, 2 * h : 2 * h + 2, :])
+            q_tiles.append(qt)
+
+        ident = keep.tile([P, P], F32, name="ident")
+        make_identity(nc, ident[:])
+        first = keep.tile([P, 1], BF16, name="first")
+        nc.gpsimd.tensor_copy(out=first[:], in_=ident[:, 0:1])
+
+        codes = {}
+        for kind in ("P", "F"):
+            c = keep.tile([P, 8, 2, P], U32, name="codes_%s" % kind, align_bytes=256)
+            s = keep.tile([P, 8, 2, P], U8, name="sc_%s" % kind, align_bytes=256)
+            codes[kind] = (c, s)
+        h_codes = {}
+        for gi in range(2):
+            for nh in range(2):
+                hc = keep.tile([P, 512], U32, name="h_codes%d%d" % (gi, nh), align_bytes=256)
+                hs = keep.tile([P, 512], U8, name="h_sc%d%d" % (gi, nh), align_bytes=256)
+                h_codes[(gi, nh)] = (hc, hs)
+
+        wide = {}
+        banks = {}
+        grouped = {}
+        hg = {}
+
+        def widen(x):
+            w = keep.tile([P, N], BF16, name="wide_%s%d" % x, align_bytes=64)
+            wide[x] = w
+            view = w[:].rearrange("p (k u w e) -> p k w u e", k=2, u=2, e=2)
+            for c in range(8):
+                src = raw[x][:, P * c : P * c + P].bitcast(FP8)
+                col = scale[x][:, c : c + 1]
+                if x in on_scalar:
+                    nc.scalar.activation(out=w[:, P * c : P * c + P], in_=src, func=COPY, scale=col)
+                else:
+                    k, q = divmod(c, 4)
+                    nc.vector.tensor_scalar(
+                        out=view[:, k, 32 * q : 32 * q + 32, :, :],
+                        in0=src.rearrange("p (w u e) -> p w u e", u=2, e=2),
+                        scalar1=col,
+                        scalar2=None,
+                        op0=MULT,
+                    )
+
+        def turn(x):
+            words = wide[x][:].bitcast(F32)
+            bank = psum.tile([P, 2, 2, P], F32, name="bank", tag="bank")
+            banks[x] = bank
+            for k in range(2):
+                for u in range(2):
+                    if x in on_scalar:
+                        w = words[:, 256 * k + u : 256 * k + 256 : 2]
+                    else:
+                        w = words[:, 256 * k + P * u : 256 * k + P * u + P]
+                    nc.tensor.transpose(bank[:, k, u, :], w, ident[:])
+
+        def empty(x):
+            gr = keep.tile([P, N], BF16, name="grouped_%s%d" % x, align_bytes=64)
+            grouped[x] = gr
+            nc.scalar.copy(
+                out=gr[:].bitcast(F32).rearrange("p (k r u) -> p k r u", k=2, u=2),
+                in_=banks[x][:].rearrange("p k u r -> p k r u"),
+            )
+
+        def quant(x):
+            c, s = codes[x[0]]
+            nc.vector.quantize_mx(
+                out=c[:, x[1], :, :].rearrange("p k m -> p (k m)").bitcast(FP8X4),
+                scales=s[:, x[1], :, :].rearrange("p k m -> p (k m)"),
+                in_=grouped[x][:],
+            )
+
+        def first_product(gi, b):
+            bank = psum.tile([P, 4, P], F32, name="bank", tag="bank")
+            banks[(gi, b)] = bank
+            pc, ps = codes["P"]
+            fc, fs = codes["F"]
+            for t in range(4):
+                for k in range(2):
+                    nc.tensor.matmul_mx(
+                        out=bank[:, t, :],
+                        lhsT=pc[:, 4 * gi + t, k, :].bitcast(FP8X4),
+                        lhsT_scale=ps[:, 4 * gi + t, k, :],
+                        rhs=fc[:, b, k, :].bitcast(FP8X4),
+                        rhs_scale=fs[:, b, k, :],
+                        start=(k == 0),
+                        stop=(k == 1),
+                    )
+
+        def gain_h(gi, b):
+            if b % 2 == 0:
+                t = keep.tile([P, 2, P, 4], BF16, name="hg_%d%d" % (gi, b), align_bytes=64)
+                hg[(gi, b // 2)] = t
+            nc.vector.tensor_tensor(
+                out=hg[(gi, b // 2)][:, b % 2, :, :],
+                in0=banks[(gi, b)][:].rearrange("p t n -> p n t"),
+                in1=g_rows[:, P * b : P * b + P].unsqueeze(2).to_broadcast([P, P, 4]),
+                op=MULT,
+            )
+
+        def quant_h(gi, b2):
+            nh, j = divmod(b2, 2)
+            c, s = h_codes[(gi, nh)]
+            nc.vector.quantize_mx(
+                out=c[:, 256 * j : 256 * j + 256].bitcast(FP8X4),
+                scales=s[:, 256 * j : 256 * j + 256],
+                in_=hg[(gi, b2)][:].rearrange("p b n t -> p (b n t)"),
+            )
+
+        def second_product(m, nh):
+            bank = psum.tile([P, 512], F32, name="bank", tag="bank")
+            banks[("o", m, nh)] = bank
+            fc, fs = codes["F"]
+            for gi in range(2):
+                c, s = h_codes[(gi, nh)]
+                nc.tensor.matmul_mx(
+                    out=bank[:],
+                    lhsT=fc[:, m, gi, :].bitcast(FP8X4),
+                    lhsT_scale=fs[:, m, gi, :],
+                    rhs=c[:].bitcast(FP8X4),
+                    rhs_scale=s[:],
+                    start=(gi == 0),
+                    stop=(gi == 1),
+                )
+
+        def finish(m, nh):
+            bank = banks[("o", m, nh)]
+            res = keep.tile([P, 512], F32, name="res_%d%d" % (m, nh))
+            q = q_tiles[m // 2][:, m % 2, 512 * nh : 512 * nh + 512]
+            if (m, nh) in on_gpsimd:
+                y = keep.tile([P, 512], F32, name="y_%d%d" % (m, nh))
+                nc.scalar.activation(out=y[:], in_=bank[:], func=COPY, scale=g_col[:, m : m + 1])
+                nc.gpsimd.tensor_tensor(out=res[:], in0=y[:], in1=q, op=ADD)
+            else:
+                nc.vector.scalar_tensor_tensor(
+                    out=res[:], in0=bank[:], scalar=g_col[:, m : m + 1], in1=q, op0=MULT, op1=ADD
+                )
+            nc.sync.dma_start(out=out[P * m : P * m + P, 512 * nh : 512 * nh + 512], in_=res[:])
+
+        for x in on_scalar:
+            widen(x)
+        for i, x in enumerate(order):
+            if i >= 8:
+                empty(order[i - 8])
+            if x not in on_scalar:
+                widen(x)
+            turn(x)
+        for x in order[8:]:
+            empty(x)
+        gain_bank = psum.tile([P, 512], F32, name="bank", tag="bank")
+        for m in range(8):
+            nc.tensor.matmul(gain_bank[:, m : m + 1], lhsT=g_rows[:, P * m : P * m + P], rhs=first[:], start=True, stop=True)
+        for x in order[:8]:
+            quant(x)
+        g_col = keep.tile([P, 8], F32, name="g_col")
+        nc.scalar.copy(out=g_col[:], in_=gain_bank[:, 0:8])
+
+        for gi in range(2):
+            for b in range(4):
+                first_product(gi, b)
+                gain_h(gi, b)
+                quant(order[8 + 4 * gi + b])
+                if b % 2 == 1:
+                    quant_h(gi, b // 2)
+        for b in range(4, 8):
+            for gi in range(2):
+                first_product(gi, b)
+            for m in (2 * (b - 4), 2 * (b - 4) + 1):
+                second_product(m, 0)
+            for gi in range(2):
+                gain_h(gi, b)
+                finish(2 * (b - 4) + gi, 0)
+                if b % 2 == 1:
+                    quant_h(gi, b // 2)
+        for m in range(8):
+            second_product(m, 1)
+            finish(m, 1)

@@ -28,8 +28,7 @@ def tile_kalman_predicted_covariance_d2_kernel(tc, P_bytes, P_scale, F_bytes, F_
 
         order = [("P", 0), ("P", 1), ("P", 2), ("P", 3), ("F", 0), ("F", 1), ("F", 2), ("F", 3)]
         order += [("P", 4), ("P", 5), ("P", 6), ("P", 7), ("F", 4), ("F", 5), ("F", 6), ("F", 7)]
-        on_scalar = [order[i] for i in range(1, 16, 4)]
-        on_gpsimd = [(1, 0), (3, 0), (5, 0), (7, 0), (0, 1), (2, 1)]
+        on_scalar = [order[i] for i in range(1, 16, 3)]
 
         p_scale = keep.tile([P, 2, 32], F32, name="p_scale")
         nc.scalar.dma_start(out=p_scale[:], in_=P_scale.rearrange("(g m t) c -> m g (t c)", g=2, t=4))
@@ -85,21 +84,13 @@ def tile_kalman_predicted_covariance_d2_kernel(tc, P_bytes, P_scale, F_bytes, F_
         def widen(x):
             w = keep.tile([P, N], BF16, name="wide_%s%d" % x, align_bytes=64)
             wide[x] = w
-            view = w[:].rearrange("p (k u w e) -> p k w u e", k=2, u=2, e=2)
             for c in range(8):
                 src = raw[x][:, P * c : P * c + P].bitcast(FP8)
                 col = scale[x][:, c : c + 1]
                 if x in on_scalar:
                     nc.scalar.activation(out=w[:, P * c : P * c + P], in_=src, func=COPY, scale=col)
                 else:
-                    k, q = divmod(c, 4)
-                    nc.vector.tensor_scalar(
-                        out=view[:, k, 32 * q : 32 * q + 32, :, :],
-                        in0=src.rearrange("p (w u e) -> p w u e", u=2, e=2),
-                        scalar1=col,
-                        scalar2=None,
-                        op0=MULT,
-                    )
+                    nc.vector.tensor_scalar(out=w[:, P * c : P * c + P], in0=src, scalar1=col, scalar2=None, op0=MULT)
 
         def turn(x):
             words = wide[x][:].bitcast(F32)
@@ -107,10 +98,7 @@ def tile_kalman_predicted_covariance_d2_kernel(tc, P_bytes, P_scale, F_bytes, F_
             banks[x] = bank
             for k in range(2):
                 for u in range(2):
-                    if x in on_scalar:
-                        w = words[:, 256 * k + u : 256 * k + 256 : 2]
-                    else:
-                        w = words[:, 256 * k + P * u : 256 * k + P * u + P]
+                    w = words[:, 256 * k + u : 256 * k + 256 : 2]
                     nc.tensor.transpose(bank[:, k, u, :], w, ident[:])
 
         def empty(x):
@@ -186,14 +174,9 @@ def tile_kalman_predicted_covariance_d2_kernel(tc, P_bytes, P_scale, F_bytes, F_
             bank = banks[("o", m, nh)]
             res = keep.tile([P, 512], F32, name="res_%d%d" % (m, nh))
             q = q_tiles[m // 2][:, m % 2, 512 * nh : 512 * nh + 512]
-            if (m, nh) in on_gpsimd:
-                y = keep.tile([P, 512], F32, name="y_%d%d" % (m, nh))
-                nc.scalar.activation(out=y[:], in_=bank[:], func=COPY, scale=g_col[:, m : m + 1])
-                nc.gpsimd.tensor_tensor(out=res[:], in0=y[:], in1=q, op=ADD)
-            else:
-                nc.vector.scalar_tensor_tensor(
-                    out=res[:], in0=bank[:], scalar=g_col[:, m : m + 1], in1=q, op0=MULT, op1=ADD
-                )
+            nc.vector.scalar_tensor_tensor(
+                out=res[:], in0=bank[:], scalar=g_col[:, m : m + 1], in1=q, op0=MULT, op1=ADD
+            )
             nc.sync.dma_start(out=out[P * m : P * m + P, 512 * nh : 512 * nh + 512], in_=res[:])
 
         for x in on_scalar:
@@ -214,23 +197,22 @@ def tile_kalman_predicted_covariance_d2_kernel(tc, P_bytes, P_scale, F_bytes, F_
         g_col = keep.tile([P, 8], F32, name="g_col")
         nc.scalar.copy(out=g_col[:], in_=gain_bank[:, 0:8])
 
-        for gi in range(2):
-            for b in range(4):
-                first_product(gi, b)
-                gain_h(gi, b)
-                quant(order[8 + 4 * gi + b])
-                if b % 2 == 1:
-                    quant_h(gi, b // 2)
-        for b in range(4, 8):
-            for gi in range(2):
-                first_product(gi, b)
-            for m in (2 * (b - 4), 2 * (b - 4) + 1):
-                second_product(m, 0)
-            for gi in range(2):
-                gain_h(gi, b)
-                finish(2 * (b - 4) + gi, 0)
-                if b % 2 == 1:
-                    quant_h(gi, b // 2)
-        for m in range(8):
-            second_product(m, 1)
-            finish(m, 1)
+        seq = [(gi, b) for gi in range(2) for b in range(4)] + [(gi, b) for gi in range(2) for b in range(4, 8)]
+        pending = None
+        for i, (gi, b) in enumerate(seq):
+            first_product(gi, b)
+            gain_h(gi, b)
+            if pending is not None:
+                quant_h(pending[0], pending[1])
+                pending = None
+            if i < 8:
+                quant(order[8 + i])
+            if b % 2 == 1:
+                pending = (gi, b // 2)
+        for nh in range(2):
+            for m in range(8):
+                second_product(m, nh)
+                finish(m, nh)
+                if pending is not None:
+                    quant_h(pending[0], pending[1])
+                    pending = None

@@ -28,7 +28,7 @@ def tile_kalman_predicted_covariance_d2_kernel(tc, P_bytes, P_scale, F_bytes, F_
 
         order = [("P", 0), ("P", 1), ("P", 2), ("P", 3), ("F", 0), ("F", 1), ("F", 2), ("F", 3)]
         order += [("P", 4), ("P", 5), ("P", 6), ("P", 7), ("F", 4), ("F", 5), ("F", 6), ("F", 7)]
-        on_scalar = [order[i] for i in range(1, 16, 3)]
+        on_scalar = [("P", 1), ("F", 1), ("P", 5), ("F", 5), ("F", 7)]
 
         p_scale = keep.tile([P, 2, 32], F32, name="p_scale")
         nc.scalar.dma_start(out=p_scale[:], in_=P_scale.rearrange("(g m t) c -> m g (t c)", g=2, t=4))
@@ -50,14 +50,15 @@ def tile_kalman_predicted_covariance_d2_kernel(tc, P_bytes, P_scale, F_bytes, F_
         for b in range(8):
             scale[("P", b)] = p_scale[:, b // 4, 8 * (b % 4) : 8 * (b % 4) + 8]
             scale[("F", b)] = f_scale[:, 8 * b : 8 * b + 8]
-        g_rows = keep.tile([P, N], BF16, name="g_rows")
-        nc.sync.dma_start(out=g_rows[:], in_=g.partition_broadcast(P))
         q_rows = Q.rearrange("(b p) n -> p b n", p=P)
         q_tiles = []
         for h in range(4):
             qt = keep.tile([P, 2, N], BF16, name="q%d" % h)
             nc.sync.dma_start(out=qt[:], in_=q_rows[:, 2 * h : 2 * h + 2, :])
             q_tiles.append(qt)
+            if h == 0:
+                g_rows = keep.tile([P, N], BF16, name="g_rows")
+                nc.sync.dma_start(out=g_rows[:], in_=g.partition_broadcast(P))
 
         ident = keep.tile([P, P], F32, name="ident")
         make_identity(nc, ident[:])
@@ -80,6 +81,7 @@ def tile_kalman_predicted_covariance_d2_kernel(tc, P_bytes, P_scale, F_bytes, F_
         banks = {}
         grouped = {}
         hg = {}
+        ht = {}
 
         def widen(x):
             w = keep.tile([P, N], BF16, name="wide_%s%d" % x, align_bytes=64)
@@ -135,14 +137,22 @@ def tile_kalman_predicted_covariance_d2_kernel(tc, P_bytes, P_scale, F_bytes, F_
                     )
 
         def gain_h(gi, b):
+            t = keep.tile([P, 4, P], BF16, name="ht_%d%d" % (gi, b), align_bytes=64)
+            ht[(gi, b)] = t
+            nc.vector.tensor_tensor(
+                out=t[:],
+                in0=banks[(gi, b)][:],
+                in1=g_rows[:, P * b : P * b + P].unsqueeze(1).to_broadcast([P, 4, P]),
+                op=MULT,
+            )
+
+        def interleave_h(gi, b):
             if b % 2 == 0:
                 t = keep.tile([P, 2, P, 4], BF16, name="hg_%d%d" % (gi, b), align_bytes=64)
                 hg[(gi, b // 2)] = t
-            nc.vector.tensor_tensor(
+            nc.scalar.copy(
                 out=hg[(gi, b // 2)][:, b % 2, :, :],
-                in0=banks[(gi, b)][:].rearrange("p t n -> p n t"),
-                in1=g_rows[:, P * b : P * b + P].unsqueeze(2).to_broadcast([P, P, 4]),
-                op=MULT,
+                in_=ht[(gi, b)][:].rearrange("p t n -> p n t"),
             )
 
         def quant_h(gi, b2):
@@ -179,40 +189,64 @@ def tile_kalman_predicted_covariance_d2_kernel(tc, P_bytes, P_scale, F_bytes, F_
             )
             nc.sync.dma_start(out=out[P * m : P * m + P, 512 * nh : 512 * nh + 512], in_=res[:])
 
-        for x in on_scalar:
+        first_half, second_half = order[:8], order[8:]
+        on_vector = [x for x in order if x not in on_scalar]
+        for x in on_scalar[:3]:
             widen(x)
-        for i, x in enumerate(order):
-            if i >= 8:
-                empty(order[i - 8])
+        for x in first_half:
             if x not in on_scalar:
                 widen(x)
             turn(x)
-        for x in order[8:]:
+        for x in on_vector[6:8]:
+            widen(x)
+        for x in first_half:
+            empty(x)
+        for x in on_scalar[3:]:
+            widen(x)
+        for x in first_half[:5]:
+            quant(x)
+        for x in on_vector[8:]:
+            widen(x)
+        for x in first_half[5:]:
+            quant(x)
+        for x in second_half[:4]:
+            turn(x)
             empty(x)
         gain_bank = psum.tile([P, 512], F32, name="bank", tag="bank")
         for m in range(8):
             nc.tensor.matmul(gain_bank[:, m : m + 1], lhsT=g_rows[:, P * m : P * m + P], rhs=first[:], start=True, stop=True)
-        for x in order[:8]:
-            quant(x)
         g_col = keep.tile([P, 8], F32, name="g_col")
         nc.scalar.copy(out=g_col[:], in_=gain_bank[:, 0:8])
 
+        for b in range(4):
+            first_product(0, b)
+        for x in second_half[4:]:
+            turn(x)
+        for x in second_half[4:6]:
+            empty(x)
         seq = [(gi, b) for gi in range(2) for b in range(4)] + [(gi, b) for gi in range(2) for b in range(4, 8)]
-        pending = None
+        ready = []
+        done = 0
         for i, (gi, b) in enumerate(seq):
-            first_product(gi, b)
+            if i >= 4:
+                first_product(gi, b)
             gain_h(gi, b)
-            if pending is not None:
-                quant_h(pending[0], pending[1])
-                pending = None
+            interleave_h(gi, b)
+            if i < 2:
+                empty(second_half[6 + i])
             if i < 8:
-                quant(order[8 + i])
+                quant(second_half[i])
             if b % 2 == 1:
-                pending = (gi, b // 2)
+                ready.append((gi, b // 2))
+            if 8 <= i < 12:
+                quant_h(ready[done][0], ready[done][1])
+                done += 1
+        n = 0
         for nh in range(2):
             for m in range(8):
                 second_product(m, nh)
                 finish(m, nh)
-                if pending is not None:
-                    quant_h(pending[0], pending[1])
-                    pending = None
+                n += 1
+                if n >= 3 and done < 8:
+                    quant_h(ready[done][0], ready[done][1])
+                    done += 1

@@ -28,7 +28,8 @@ def tile_kalman_predicted_covariance_d2_kernel(tc, P_bytes, P_scale, F_bytes, F_
 
         order = [("P", 0), ("P", 1), ("P", 2), ("P", 3), ("F", 0), ("F", 1), ("F", 2), ("F", 3)]
         order += [("P", 4), ("P", 5), ("P", 6), ("P", 7), ("F", 4), ("F", 5), ("F", 6), ("F", 7)]
-        on_scalar = [("P", 1), ("F", 1), ("P", 5), ("F", 5), ("F", 7)]
+        on_scalar = [("P", 1), ("F", 1), ("P", 5), ("P", 7), ("F", 5), ("F", 7)]
+        on_gpsimd = []
 
         p_scale = keep.tile([P, 2, 32], F32, name="p_scale")
         nc.scalar.dma_start(out=p_scale[:], in_=P_scale.rearrange("(g m t) c -> m g (t c)", g=2, t=4))
@@ -38,15 +39,13 @@ def tile_kalman_predicted_covariance_d2_kernel(tc, P_bytes, P_scale, F_bytes, F_
         f_rows = F_bytes.rearrange("(b p) j -> p b j", p=P)
         raw = {}
         scale = {}
-        for i in range(0, 16, 2):
+        for i, n in [(0, 1), (1, 1)] + [(i, 2) for i in range(2, 16, 2)]:
             kind, b = order[i]
-            pair = keep.tile([P, 2, N], U8, name="bytes_%s%d" % (kind, b))
-            if kind == "P":
-                nc.sync.dma_start(out=pair[:], in_=p_rows[b // 4][:, b % 4 : b % 4 + 2, :])
-            else:
-                nc.sync.dma_start(out=pair[:], in_=f_rows[:, b : b + 2, :])
-            for j in range(2):
-                raw[order[i + j]] = pair[:, j, :]
+            part = keep.tile([P, n, N], U8, name="bytes_%s%d" % (kind, b))
+            rows = p_rows[b // 4][:, b % 4 : b % 4 + n, :] if kind == "P" else f_rows[:, b : b + n, :]
+            nc.sync.dma_start(out=part[:], in_=rows)
+            for j in range(n):
+                raw[order[i + j]] = part[:, j, :]
         for b in range(8):
             scale[("P", b)] = p_scale[:, b // 4, 8 * (b % 4) : 8 * (b % 4) + 8]
             scale[("F", b)] = f_scale[:, 8 * b : 8 * b + 8]
@@ -104,19 +103,22 @@ def tile_kalman_predicted_covariance_d2_kernel(tc, P_bytes, P_scale, F_bytes, F_
                     nc.tensor.transpose(bank[:, k, u, :], w, ident[:])
 
         def empty(x):
-            gr = keep.tile([P, N], BF16, name="grouped_%s%d" % x, align_bytes=64)
-            grouped[x] = gr
+            kind, b = x
+            if b % 2 == 0:
+                gr = keep.tile([P, 2, N], BF16, name="grouped_%s%d" % x, align_bytes=64)
+                grouped[(kind, b // 2)] = gr
             nc.scalar.copy(
-                out=gr[:].bitcast(F32).rearrange("p (k r u) -> p k r u", k=2, u=2),
+                out=grouped[(kind, b // 2)][:, b % 2, :].bitcast(F32).rearrange("p (k r u) -> p k r u", k=2, u=2),
                 in_=banks[x][:].rearrange("p k u r -> p k r u"),
             )
 
-        def quant(x):
-            c, s = codes[x[0]]
+        def quant(kind, pair):
+            c, s = codes[kind]
+            b = 2 * pair
             nc.vector.quantize_mx(
-                out=c[:, x[1], :, :].rearrange("p k m -> p (k m)").bitcast(FP8X4),
-                scales=s[:, x[1], :, :].rearrange("p k m -> p (k m)"),
-                in_=grouped[x][:],
+                out=c[:, b : b + 2, :, :].rearrange("p b k m -> p (b k m)").bitcast(FP8X4),
+                scales=s[:, b : b + 2, :, :].rearrange("p b k m -> p (b k m)"),
+                in_=grouped[(kind, pair)][:].rearrange("p b c -> p (b c)"),
             )
 
         def first_product(gi, b):
@@ -151,8 +153,8 @@ def tile_kalman_predicted_covariance_d2_kernel(tc, P_bytes, P_scale, F_bytes, F_
                 t = keep.tile([P, 2, P, 4], BF16, name="hg_%d%d" % (gi, b), align_bytes=64)
                 hg[(gi, b // 2)] = t
             nc.scalar.copy(
-                out=hg[(gi, b // 2)][:, b % 2, :, :],
-                in_=ht[(gi, b)][:].rearrange("p t n -> p n t"),
+                out=hg[(gi, b // 2)][:, b % 2, :, :].rearrange("p (c i) t -> p c t i", i=4),
+                in_=ht[(gi, b)][:].rearrange("p t (c i) -> p c t i", i=4),
             )
 
         def quant_h(gi, b2):
@@ -184,62 +186,65 @@ def tile_kalman_predicted_covariance_d2_kernel(tc, P_bytes, P_scale, F_bytes, F_
             bank = banks[("o", m, nh)]
             res = keep.tile([P, 512], F32, name="res_%d%d" % (m, nh))
             q = q_tiles[m // 2][:, m % 2, 512 * nh : 512 * nh + 512]
-            nc.vector.scalar_tensor_tensor(
-                out=res[:], in0=bank[:], scalar=g_col[:, m : m + 1], in1=q, op0=MULT, op1=ADD
-            )
+            if (m, nh) in on_gpsimd:
+                y = keep.tile([P, 512], F32, name="y_%d%d" % (m, nh))
+                nc.scalar.activation(out=y[:], in_=bank[:], func=COPY, scale=g_col[:, m : m + 1])
+                nc.gpsimd.tensor_tensor(out=res[:], in0=y[:], in1=q, op=ADD)
+            else:
+                nc.vector.scalar_tensor_tensor(
+                    out=res[:], in0=bank[:], scalar=g_col[:, m : m + 1], in1=q, op0=MULT, op1=ADD
+                )
             nc.sync.dma_start(out=out[P * m : P * m + P, 512 * nh : 512 * nh + 512], in_=res[:])
 
-        first_half, second_half = order[:8], order[8:]
         on_vector = [x for x in order if x not in on_scalar]
-        for x in on_scalar[:3]:
+        for x in on_scalar[:4]:
             widen(x)
-        for x in first_half:
-            if x not in on_scalar:
-                widen(x)
+        for x in on_vector[:9]:
+            widen(x)
+        for x in order[:8]:
             turn(x)
-        for x in on_vector[6:8]:
-            widen(x)
-        for x in first_half:
+        for x in order[:6]:
             empty(x)
-        for x in on_scalar[3:]:
-            widen(x)
-        for x in first_half[:5]:
-            quant(x)
-        for x in on_vector[8:]:
-            widen(x)
-        for x in first_half[5:]:
-            quant(x)
-        for x in second_half[:4]:
+        widen(on_scalar[4])
+        for x in order[8:12]:
             turn(x)
+        for x in order[6:12]:
+            empty(x)
+        widen(on_scalar[5])
+        for x in order[12:14]:
+            turn(x)
+        for x in order[12:14]:
             empty(x)
         gain_bank = psum.tile([P, 512], F32, name="bank", tag="bank")
         for m in range(8):
             nc.tensor.matmul(gain_bank[:, m : m + 1], lhsT=g_rows[:, P * m : P * m + P], rhs=first[:], start=True, stop=True)
+        quant("P", 0)
+        quant("P", 1)
+        quant("F", 0)
+        widen(on_vector[9])
+        quant("F", 1)
+        for b in range(4):
+            first_product(0, b)
+        for x in order[14:]:
+            turn(x)
+        for x in order[14:]:
+            empty(x)
         g_col = keep.tile([P, 8], F32, name="g_col")
         nc.scalar.copy(out=g_col[:], in_=gain_bank[:, 0:8])
 
-        for b in range(4):
-            first_product(0, b)
-        for x in second_half[4:]:
-            turn(x)
-        for x in second_half[4:6]:
-            empty(x)
         seq = [(gi, b) for gi in range(2) for b in range(4)] + [(gi, b) for gi in range(2) for b in range(4, 8)]
-        ready = []
+        late = [("P", 2), ("P", 3), ("F", 2), ("F", 3)]
+        pairs = [(gi, b // 2) for gi, b in seq if b % 2 == 0]
         done = 0
         for i, (gi, b) in enumerate(seq):
             if i >= 4:
                 first_product(gi, b)
             gain_h(gi, b)
             interleave_h(gi, b)
-            if i < 2:
-                empty(second_half[6 + i])
-            if i < 8:
-                quant(second_half[i])
-            if b % 2 == 1:
-                ready.append((gi, b // 2))
-            if 8 <= i < 12:
-                quant_h(ready[done][0], ready[done][1])
+            if i < 4:
+                quant(late[i][0], late[i][1])
+            if i >= 4 and i % 2 == 0:
+                quant_h(pairs[done][0], pairs[done][1])
                 done += 1
         n = 0
         for nh in range(2):
@@ -247,6 +252,6 @@ def tile_kalman_predicted_covariance_d2_kernel(tc, P_bytes, P_scale, F_bytes, F_
                 second_product(m, nh)
                 finish(m, nh)
                 n += 1
-                if n >= 3 and done < 8:
-                    quant_h(ready[done][0], ready[done][1])
+                if n >= 2 and done < 8:
+                    quant_h(pairs[done][0], pairs[done][1])
                     done += 1

@@ -28,7 +28,7 @@ def tile_kalman_predicted_covariance_d2_kernel(tc, P_bytes, P_scale, F_bytes, F_
 
         order = [("P", 0), ("P", 1), ("P", 2), ("P", 3), ("F", 0), ("F", 1), ("F", 2), ("F", 3)]
         order += [("P", 4), ("P", 5), ("P", 6), ("P", 7), ("F", 4), ("F", 5), ("F", 6), ("F", 7)]
-        on_scalar = [("P", 1), ("F", 1), ("P", 5), ("P", 7), ("F", 5), ("F", 7)]
+        on_scalar = [("P", 1), ("F", 1), ("P", 5), ("F", 7)]
         on_gpsimd = []
 
         p_scale = keep.tile([P, 2, 32], F32, name="p_scale")
@@ -65,10 +65,12 @@ def tile_kalman_predicted_covariance_d2_kernel(tc, P_bytes, P_scale, F_bytes, F_
         nc.gpsimd.tensor_copy(out=first[:], in_=ident[:, 0:1])
 
         codes = {}
-        for kind in ("P", "F"):
-            c = keep.tile([P, 8, 2, P], U32, name="codes_%s" % kind, align_bytes=256)
-            s = keep.tile([P, 8, 2, P], U8, name="sc_%s" % kind, align_bytes=256)
-            codes[kind] = (c, s)
+        c = keep.tile([P, 8, 2, P], U32, name="codes_P", align_bytes=256)
+        s = keep.tile([P, 8, 2, P], U8, name="sc_P", align_bytes=256)
+        codes["P"] = (c, s)
+        c = keep.tile([P, 2, 2, 512], U32, name="codes_F", align_bytes=256)
+        s = keep.tile([P, 2, 2, 512], U8, name="sc_F", align_bytes=256)
+        codes["F"] = (c, s)
         h_codes = {}
         for gi in range(2):
             for nh in range(2):
@@ -104,66 +106,79 @@ def tile_kalman_predicted_covariance_d2_kernel(tc, P_bytes, P_scale, F_bytes, F_
 
         def empty(x):
             kind, b = x
-            if b % 2 == 0:
-                gr = keep.tile([P, 2, N], BF16, name="grouped_%s%d" % x, align_bytes=64)
-                grouped[(kind, b // 2)] = gr
+            if kind == "P":
+                if b % 2 == 0:
+                    gr = keep.tile([P, 2, 2, 512], BF16, name="grouped_P%d" % b, align_bytes=64)
+                    grouped[("P", b // 2)] = gr
+                dst = grouped[("P", b // 2)][:, b % 2, :, :]
+            else:
+                if b % 4 == 0:
+                    gr = keep.tile([P, 2, 4, 512], BF16, name="grouped_F%d" % b, align_bytes=64)
+                    grouped[("F", b // 4)] = gr
+                dst = grouped[("F", b // 4)][:, :, b % 4, :]
             nc.scalar.copy(
-                out=grouped[(kind, b // 2)][:, b % 2, :].bitcast(F32).rearrange("p (k r u) -> p k r u", k=2, u=2),
+                out=dst.bitcast(F32).rearrange("p k (r u) -> p k r u", u=2),
                 in_=banks[x][:].rearrange("p k u r -> p k r u"),
             )
 
-        def quant(kind, pair):
-            c, s = codes[kind]
+        def quant_p(pair):
+            c, s = codes["P"]
             b = 2 * pair
             nc.vector.quantize_mx(
                 out=c[:, b : b + 2, :, :].rearrange("p b k m -> p (b k m)").bitcast(FP8X4),
                 scales=s[:, b : b + 2, :, :].rearrange("p b k m -> p (b k m)"),
-                in_=grouped[(kind, pair)][:].rearrange("p b c -> p (b c)"),
+                in_=grouped[("P", pair)][:].rearrange("p b k c -> p (b k c)"),
             )
 
-        def first_product(gi, b):
-            bank = psum.tile([P, 4, P], F32, name="bank", tag="bank")
-            banks[(gi, b)] = bank
+        def quant_f(nh, k):
+            c, s = codes["F"]
+            nc.vector.quantize_mx(
+                out=c[:, nh, k, :].bitcast(FP8X4),
+                scales=s[:, nh, k, :],
+                in_=grouped[("F", nh)][:, k, :, :].rearrange("p b c -> p (b c)"),
+            )
+
+        def first_product(gi, nh, t):
+            bank = psum.tile([P, 512], F32, name="bank", tag="bank")
+            banks[(gi, nh, t)] = bank
             pc, ps = codes["P"]
             fc, fs = codes["F"]
-            for t in range(4):
-                for k in range(2):
-                    nc.tensor.matmul_mx(
-                        out=bank[:, t, :],
-                        lhsT=pc[:, 4 * gi + t, k, :].bitcast(FP8X4),
-                        lhsT_scale=ps[:, 4 * gi + t, k, :],
-                        rhs=fc[:, b, k, :].bitcast(FP8X4),
-                        rhs_scale=fs[:, b, k, :],
-                        start=(k == 0),
-                        stop=(k == 1),
-                    )
+            for k in range(2):
+                nc.tensor.matmul_mx(
+                    out=bank[:],
+                    lhsT=pc[:, 4 * gi + t, k, :].bitcast(FP8X4),
+                    lhsT_scale=ps[:, 4 * gi + t, k, :],
+                    rhs=fc[:, nh, k, :].bitcast(FP8X4),
+                    rhs_scale=fs[:, nh, k, :],
+                    start=(k == 0),
+                    stop=(k == 1),
+                )
 
-        def gain_h(gi, b):
-            t = keep.tile([P, 4, P], BF16, name="ht_%d%d" % (gi, b), align_bytes=64)
-            ht[(gi, b)] = t
+        def gain_h(gi, nh, t):
+            if t == 0:
+                tile_ht = keep.tile([P, 4, 512], BF16, name="ht_%d%d" % (gi, nh), align_bytes=64)
+                ht[(gi, nh)] = tile_ht
             nc.vector.tensor_tensor(
-                out=t[:],
-                in0=banks[(gi, b)][:],
-                in1=g_rows[:, P * b : P * b + P].unsqueeze(1).to_broadcast([P, 4, P]),
+                out=ht[(gi, nh)][:, t, :],
+                in0=banks[(gi, nh, t)][:],
+                in1=g_rows[:, 512 * nh : 512 * nh + 512],
                 op=MULT,
             )
 
-        def interleave_h(gi, b):
-            if b % 2 == 0:
-                t = keep.tile([P, 2, P, 4], BF16, name="hg_%d%d" % (gi, b), align_bytes=64)
-                hg[(gi, b // 2)] = t
+        def interleave_h(gi, nh, j):
+            tile_hg = keep.tile([P, 256, 4], BF16, name="hg_%d%d%d" % (gi, nh, j), align_bytes=64)
+            hg[(gi, nh, j)] = tile_hg
             nc.scalar.copy(
-                out=hg[(gi, b // 2)][:, b % 2, :, :].rearrange("p (c i) t -> p c t i", i=4),
-                in_=ht[(gi, b)][:].rearrange("p t (c i) -> p c t i", i=4),
+                out=tile_hg[:].rearrange("p (c i) t -> p c t i", i=4),
+                in_=ht[(gi, nh)][:, :, 256 * j : 256 * j + 256].rearrange("p t (c i) -> p c t i", i=4),
             )
 
-        def quant_h(gi, b2):
-            nh, j = divmod(b2, 2)
+        def quant_h(gi, nh, j):
             c, s = h_codes[(gi, nh)]
             nc.vector.quantize_mx(
                 out=c[:, 256 * j : 256 * j + 256].bitcast(FP8X4),
                 scales=s[:, 256 * j : 256 * j + 256],
-                in_=hg[(gi, b2)][:].rearrange("p b n t -> p (b n t)"),
+                in_=hg[(gi, nh, j)][:].rearrange("p n t -> p (n t)"),
             )
 
         def second_product(m, nh):
@@ -174,8 +189,8 @@ def tile_kalman_predicted_covariance_d2_kernel(tc, P_bytes, P_scale, F_bytes, F_
                 c, s = h_codes[(gi, nh)]
                 nc.tensor.matmul_mx(
                     out=bank[:],
-                    lhsT=fc[:, m, gi, :].bitcast(FP8X4),
-                    lhsT_scale=fs[:, m, gi, :],
+                    lhsT=fc[:, m // 4, gi, P * (m % 4) : P * (m % 4) + P].bitcast(FP8X4),
+                    lhsT_scale=fs[:, m // 4, gi, P * (m % 4) : P * (m % 4) + P],
                     rhs=c[:].bitcast(FP8X4),
                     rhs_scale=s[:],
                     start=(gi == 0),
@@ -197,54 +212,53 @@ def tile_kalman_predicted_covariance_d2_kernel(tc, P_bytes, P_scale, F_bytes, F_
             nc.sync.dma_start(out=out[P * m : P * m + P, 512 * nh : 512 * nh + 512], in_=res[:])
 
         on_vector = [x for x in order if x not in on_scalar]
-        for x in on_scalar[:4]:
+        for x in on_scalar[:3]:
             widen(x)
-        for x in on_vector[:9]:
+        for x in on_vector[:10]:
             widen(x)
         for x in order[:8]:
             turn(x)
-        for x in order[:6]:
+        for x in order[:8]:
             empty(x)
-        widen(on_scalar[4])
+        for x in order[8:13]:
+            turn(x)
         for x in order[8:12]:
-            turn(x)
-        for x in order[6:12]:
             empty(x)
-        widen(on_scalar[5])
-        for x in order[12:14]:
-            turn(x)
-        for x in order[12:14]:
-            empty(x)
+        widen(on_scalar[3])
+        quant_p(0)
+        quant_p(1)
+        widen(on_vector[10])
+        quant_f(0, 0)
+        quant_f(0, 1)
+        widen(on_vector[11])
+        empty(order[12])
         gain_bank = psum.tile([P, 512], F32, name="bank", tag="bank")
         for m in range(8):
             nc.tensor.matmul(gain_bank[:, m : m + 1], lhsT=g_rows[:, P * m : P * m + P], rhs=first[:], start=True, stop=True)
-        quant("P", 0)
-        quant("P", 1)
-        quant("F", 0)
-        widen(on_vector[9])
-        quant("F", 1)
-        for b in range(4):
-            first_product(0, b)
-        for x in order[14:]:
+        for t in range(4):
+            first_product(0, 0, t)
+        for x in order[13:]:
             turn(x)
-        for x in order[14:]:
+        for x in order[13:]:
             empty(x)
         g_col = keep.tile([P, 8], F32, name="g_col")
         nc.scalar.copy(out=g_col[:], in_=gain_bank[:, 0:8])
 
-        seq = [(gi, b) for gi in range(2) for b in range(4)] + [(gi, b) for gi in range(2) for b in range(4, 8)]
-        late = [("P", 2), ("P", 3), ("F", 2), ("F", 3)]
-        pairs = [(gi, b // 2) for gi, b in seq if b % 2 == 0]
+        inputs = [(quant_p, (2,)), (quant_p, (3,)), None, None, (quant_f, (1, 0)), (quant_f, (1, 1))]
+        halves = [(gi, nh, j) for nh in range(2) for gi in range(2) for j in range(2)]
         done = 0
-        for i, (gi, b) in enumerate(seq):
+        for i in range(16):
+            gi, nh, t = (i // 4) % 2, i // 8, i % 4
             if i >= 4:
-                first_product(gi, b)
-            gain_h(gi, b)
-            interleave_h(gi, b)
-            if i < 4:
-                quant(late[i][0], late[i][1])
-            if i >= 4 and i % 2 == 0:
-                quant_h(pairs[done][0], pairs[done][1])
+                first_product(gi, nh, t)
+            gain_h(gi, nh, t)
+            if t == 3:
+                interleave_h(gi, nh, 0)
+                interleave_h(gi, nh, 1)
+            if i < len(inputs) and inputs[i] is not None:
+                inputs[i][0](*inputs[i][1])
+            if i >= 7 and i % 2 == 1:
+                quant_h(*halves[done])
                 done += 1
         n = 0
         for nh in range(2):
@@ -252,6 +266,6 @@ def tile_kalman_predicted_covariance_d2_kernel(tc, P_bytes, P_scale, F_bytes, F_
                 second_product(m, nh)
                 finish(m, nh)
                 n += 1
-                if n >= 2 and done < 8:
-                    quant_h(pairs[done][0], pairs[done][1])
+                if n >= 3 and done < 8:
+                    quant_h(*halves[done])
                     done += 1

from contextlib import ExitStack

import concourse.mybir as mybir
from concourse.masks import make_identity

N = 1024
P = 128
FLOPS = 2 * 2 * N * N * N

F32 = mybir.dt.float32
BF16 = mybir.dt.bfloat16
U32 = mybir.dt.uint32
U8 = mybir.dt.uint8
FP8 = mybir.dt.float8_e4m3fn
FP8X4 = mybir.dt.float8_e4m3fn_x4
MULT = mybir.AluOpType.mult
ADD = mybir.AluOpType.add
COPY = mybir.ActivationFunctionType.Copy


def tile_kalman_predicted_covariance_d2_kernel(tc, P_bytes, P_scale, F_bytes, F_scale, g, Q, out):
    nc = tc.nc
    with ExitStack() as ctx:
        keep = ctx.enter_context(tc.tile_pool(name="keep", bufs=1))
        psum = ctx.enter_context(tc.psum_pool(name="psum", bufs=8))
        ctx.enter_context(tc.manual_schedule())


        order = [("P", 0), ("P", 1), ("P", 2), ("P", 3), ("F", 0), ("F", 1), ("F", 2), ("F", 3)]
        order += [("P", 4), ("P", 5), ("P", 6), ("P", 7), ("F", 4), ("F", 5), ("F", 6), ("F", 7)]
        on_scalar = [("P", 1), ("F", 1), ("P", 5), ("F", 7)]
        on_gpsimd = []

        p_scale = keep.tile([P, 2, 32], F32, name="p_scale")
        nc.scalar.dma_start(out=p_scale[:], in_=P_scale.rearrange("(g m t) c -> m g (t c)", g=2, t=4))
        f_scale = keep.tile([P, 64], F32, name="f_scale")
        nc.scalar.dma_start(out=f_scale[:], in_=F_scale.rearrange("b c -> (b c)").partition_broadcast(P))
        p_rows = P_bytes.rearrange("(g m t) j -> g m t j", g=2, t=4)
        f_rows = F_bytes.rearrange("(b p) j -> p b j", p=P)
        raw = {}
        scale = {}
        for i, n in [(0, 1), (1, 1)] + [(i, 2) for i in range(2, 16, 2)]:
            kind, b = order[i]
            part = keep.tile([P, n, N], U8, name="bytes_%s%d" % (kind, b))
            rows = p_rows[b // 4][:, b % 4 : b % 4 + n, :] if kind == "P" else f_rows[:, b : b + n, :]
            nc.sync.dma_start(out=part[:], in_=rows)
            for j in range(n):
                raw[order[i + j]] = part[:, j, :]
        for b in range(8):
            scale[("P", b)] = p_scale[:, b // 4, 8 * (b % 4) : 8 * (b % 4) + 8]
            scale[("F", b)] = f_scale[:, 8 * b : 8 * b + 8]
        q_rows = Q.rearrange("(b p) n -> p b n", p=P)
        q_tiles = []
        for h in range(4):
            qt = keep.tile([P, 2, N], BF16, name="q%d" % h)
            nc.sync.dma_start(out=qt[:], in_=q_rows[:, 2 * h : 2 * h + 2, :])
            q_tiles.append(qt)
            if h == 0:
                g_rows = keep.tile([P, N], BF16, name="g_rows")
                nc.sync.dma_start(out=g_rows[:], in_=g.partition_broadcast(P))

        ident = keep.tile([P, P], F32, name="ident")
        make_identity(nc, ident[:])
        first = keep.tile([P, 1], BF16, name="first")
        nc.gpsimd.tensor_copy(out=first[:], in_=ident[:, 0:1])

        codes = {}
        c = keep.tile([P, 8, 2, P], U32, name="codes_P", align_bytes=256)
        s = keep.tile([P, 8, 2, P], U8, name="sc_P", align_bytes=256)
        codes["P"] = (c, s)
        c = keep.tile([P, 2, 2, 512], U32, name="codes_F", align_bytes=256)
        s = keep.tile([P, 2, 2, 512], U8, name="sc_F", align_bytes=256)
        codes["F"] = (c, s)
        h_codes = {}
        for gi in range(2):
            for nh in range(2):
                hc = keep.tile([P, 512], U32, name="h_codes%d%d" % (gi, nh), align_bytes=256)
                hs = keep.tile([P, 512], U8, name="h_sc%d%d" % (gi, nh), align_bytes=256)
                h_codes[(gi, nh)] = (hc, hs)

        wide = {}
        banks = {}
        grouped = {}
        hg = {}
        ht = {}

        def widen(x):
            w = keep.tile([P, N], BF16, name="wide_%s%d" % x, align_bytes=64)
            wide[x] = w
            for c in range(8):
                src = raw[x][:, P * c : P * c + P].bitcast(FP8)
                col = scale[x][:, c : c + 1]
                if x in on_scalar:
                    nc.scalar.activation(out=w[:, P * c : P * c + P], in_=src, func=COPY, scale=col)
                else:
                    nc.vector.tensor_scalar(out=w[:, P * c : P * c + P], in0=src, scalar1=col, scalar2=None, op0=MULT)

        def turn(x):
            words = wide[x][:].bitcast(F32)
            bank = psum.tile([P, 2, 2, P], F32, name="bank", tag="bank")
            banks[x] = bank
            for k in range(2):
                for u in range(2):
                    w = words[:, 256 * k + u : 256 * k + 256 : 2]
                    nc.tensor.transpose(bank[:, k, u, :], w, ident[:])

        def empty(x):
            kind, b = x
            if kind == "P":
                if b % 2 == 0:
                    gr = keep.tile([P, 2, 2, 512], BF16, name="grouped_P%d" % b, align_bytes=64)
                    grouped[("P", b // 2)] = gr
                dst = grouped[("P", b // 2)][:, b % 2, :, :]
            else:
                if b % 4 == 0:
                    gr = keep.tile([P, 2, 4, 512], BF16, name="grouped_F%d" % b, align_bytes=64)
                    grouped[("F", b // 4)] = gr
                dst = grouped[("F", b // 4)][:, :, b % 4, :]
            nc.scalar.copy(
                out=dst.bitcast(F32).rearrange("p k (r u) -> p k r u", u=2),
                in_=banks[x][:].rearrange("p k u r -> p k r u"),
            )

        def quant_p(pair):
            c, s = codes["P"]
            b = 2 * pair
            nc.vector.quantize_mx(
                out=c[:, b : b + 2, :, :].rearrange("p b k m -> p (b k m)").bitcast(FP8X4),
                scales=s[:, b : b + 2, :, :].rearrange("p b k m -> p (b k m)"),
                in_=grouped[("P", pair)][:].rearrange("p b k c -> p (b k c)"),
            )

        def quant_f(nh, k):
            c, s = codes["F"]
            nc.vector.quantize_mx(
                out=c[:, nh, k, :].bitcast(FP8X4),
                scales=s[:, nh, k, :],
                in_=grouped[("F", nh)][:, k, :, :].rearrange("p b c -> p (b c)"),
            )

        def first_product(gi, nh, t):
            bank = psum.tile([P, 512], F32, name="bank", tag="bank")
            banks[(gi, nh, t)] = bank
            pc, ps = codes["P"]
            fc, fs = codes["F"]
            for k in range(2):
                nc.tensor.matmul_mx(
                    out=bank[:],
                    lhsT=pc[:, 4 * gi + t, k, :].bitcast(FP8X4),
                    lhsT_scale=ps[:, 4 * gi + t, k, :],
                    rhs=fc[:, nh, k, :].bitcast(FP8X4),
                    rhs_scale=fs[:, nh, k, :],
                    start=(k == 0),
                    stop=(k == 1),
                )

        def gain_h(gi, nh, t):
            if t == 0:
                tile_ht = keep.tile([P, 4, 512], BF16, name="ht_%d%d" % (gi, nh), align_bytes=64)
                ht[(gi, nh)] = tile_ht
            nc.vector.tensor_tensor(
                out=ht[(gi, nh)][:, t, :],
                in0=banks[(gi, nh, t)][:],
                in1=g_rows[:, 512 * nh : 512 * nh + 512],
                op=MULT,
            )

        def interleave_h(gi, nh, j):
            tile_hg = keep.tile([P, 256, 4], BF16, name="hg_%d%d%d" % (gi, nh, j), align_bytes=64)
            hg[(gi, nh, j)] = tile_hg
            nc.scalar.copy(
                out=tile_hg[:].rearrange("p (c i) t -> p c t i", i=4),
                in_=ht[(gi, nh)][:, :, 256 * j : 256 * j + 256].rearrange("p t (c i) -> p c t i", i=4),
            )

        def quant_h(gi, nh, j):
            c, s = h_codes[(gi, nh)]
            nc.vector.quantize_mx(
                out=c[:, 256 * j : 256 * j + 256].bitcast(FP8X4),
                scales=s[:, 256 * j : 256 * j + 256],
                in_=hg[(gi, nh, j)][:].rearrange("p n t -> p (n t)"),
            )

        def second_product(m, nh):
            bank = psum.tile([P, 512], F32, name="bank", tag="bank")
            banks[("o", m, nh)] = bank
            fc, fs = codes["F"]
            for gi in range(2):
                c, s = h_codes[(gi, nh)]
                nc.tensor.matmul_mx(
                    out=bank[:],
                    lhsT=fc[:, m // 4, gi, P * (m % 4) : P * (m % 4) + P].bitcast(FP8X4),
                    lhsT_scale=fs[:, m // 4, gi, P * (m % 4) : P * (m % 4) + P],
                    rhs=c[:].bitcast(FP8X4),
                    rhs_scale=s[:],
                    start=(gi == 0),
                    stop=(gi == 1),
                )

        def finish(m, nh):
            bank = banks[("o", m, nh)]
            res = keep.tile([P, 512], F32, name="res_%d%d" % (m, nh))
            q = q_tiles[m // 2][:, m % 2, 512 * nh : 512 * nh + 512]
            if (m, nh) in on_gpsimd:
                y = keep.tile([P, 512], F32, name="y_%d%d" % (m, nh))
                nc.scalar.activation(out=y[:], in_=bank[:], func=COPY, scale=g_col[:, m : m + 1])
                nc.gpsimd.tensor_tensor(out=res[:], in0=y[:], in1=q, op=ADD)
            else:
                nc.vector.scalar_tensor_tensor(
                    out=res[:], in0=bank[:], scalar=g_col[:, m : m + 1], in1=q, op0=MULT, op1=ADD
                )
            nc.sync.dma_start(out=out[P * m : P * m + P, 512 * nh : 512 * nh + 512], in_=res[:])

        on_vector = [x for x in order if x not in on_scalar]
        for x in on_scalar[:3]:
            widen(x)
        for x in on_vector[:10]:
            widen(x)
        for x in order[:8]:
            turn(x)
        for x in order[:8]:
            empty(x)
        for x in order[8:13]:
            turn(x)
        for x in order[8:12]:
            empty(x)
        widen(on_scalar[3])
        quant_p(0)
        quant_p(1)
        widen(on_vector[10])
        quant_f(0, 0)
        quant_f(0, 1)
        widen(on_vector[11])
        empty(order[12])
        gain_bank = psum.tile([P, 512], F32, name="bank", tag="bank")
        for m in range(8):
            nc.tensor.matmul(gain_bank[:, m : m + 1], lhsT=g_rows[:, P * m : P * m + P], rhs=first[:], start=True, stop=True)
        for t in range(4):
            first_product(0, 0, t)
        for x in order[13:]:
            turn(x)
        for x in order[13:]:
            empty(x)
        g_col = keep.tile([P, 8], F32, name="g_col")
        nc.scalar.copy(out=g_col[:], in_=gain_bank[:, 0:8])

        inputs = [(quant_p, (2,)), (quant_p, (3,)), None, None, (quant_f, (1, 0)), (quant_f, (1, 1))]
        halves = [(gi, nh, j) for nh in range(2) for gi in range(2) for j in range(2)]
        done = 0
        for i in range(16):
            gi, nh, t = (i // 4) % 2, i // 8, i % 4
            if i >= 4:
                first_product(gi, nh, t)
            gain_h(gi, nh, t)
            if t == 3:
                interleave_h(gi, nh, 0)
                interleave_h(gi, nh, 1)
            if i < len(inputs) and inputs[i] is not None:
                inputs[i][0](*inputs[i][1])
            if i >= 7 and i % 2 == 1:
                quant_h(*halves[done])
                done += 1
        n = 0
        for nh in range(2):
            for m in range(8):
                second_product(m, nh)
                finish(m, nh)
                n += 1
                if n >= 3 and done < 8:
                    quant_h(*halves[done])
                    done += 1
